import numpy as np
CORES = [60,61,62,63,176,177,178]
N = 7
def setup_inputs(rng):
    return {"x": rng.standard_normal((N, 128, 512), dtype=np.float32)}
def reference(x):
    s = x.sum(axis=0, dtype=np.float64).astype(x.dtype)
    return {"y": np.broadcast_to(s, (N,) + s.shape)}

from concourse.bass import DstId, RemoteDMATransfer

RPC = 8
NCH = 128 // RPC
W = RPC * 512 // 128
PI = 2.5
OFF = {"conA": 1.0, "crA": 7.6, "conB": 1.0, "crB": 9.6, "up": 3.0, "down": 7.5,
       "m2f": 3.0, "fin": 4.0, "spr": 5.0, "cl": 6.0, "cs": 7.0}

SCRATCH = {"buf": ("dram", [4, 128, W], "float32")}
SEMAPHORES = ["ld", "xr", "lz", "bl", "aL", "aSA", "aSB", "aF", "aR0", "aR1", "st0", "st1", "stA", "stB",
              "cR0", "cR1", "cL", "cSA", "aLX0", "aLX1", "aLX2", "aX0", "aX1", "aX2", "sx0", "sx1", "sx2"]


def _pop(m):
    return bin(m).count("1")


def rank_program(g, core, T, topo):
    if T.rank_of(core) is None:
        return
    S, buf, n = T.sem, T.buf, NCH
    chips = {}
    for c in T.cores:
        chips.setdefault((topo.host(c), topo.chip(c)), []).append(c)
    s0, s1 = list(chips.values())

    def gates(s, o):
        return [c for c in s if all(topo.may_write(c, d) for d in o)]

    A, B = (s0, s1) if len(gates(s0, s1)) >= 2 else (s1, s0)
    gA = gates(A, B)[:2]
    pA = [c for c in A if c not in gA]
    gB = gates(B, A)[0]
    pB = [c for c in B if c != gB]

    def xc(t, c):
        return t[c * RPC:(c + 1) * RPC, :]

    def did(d):
        rid, pid = topo.addr(d, core)
        return DstId(rid=rid, pnc=pid)

    lz = [0]
    ev = []

    def plan(kind, c, fn):
        ev.append((c * PI + OFF[kind], len(ev), fn, c))

    def play():
        for _, _, fn, c in sorted(ev, key=lambda e: (e[0], e[1])):
            fn(c)

    def copy(src, d, slot, rsem, lsem):
        rid, pid = topo.addr(d, core)
        g.remote_dma(out_ap=buf[slot], in_ap=buf[src], remote_sem=rsem, local_sem=lsem, pid=pid, routing_id=rid,
                     dma_engine_mask=topo.mask(core, d))

    def fold(srcs, d, slot, rsem, lsem):
        g.remote_dma_fused([RemoteDMATransfer(dst_ids=[did(d)], dma_engine_mask=topo.mask(core, d), remote_sem=rsem,
                                              srcs=[buf[s] for s in srcs], dsts=[buf[slot]], alu_op=1)], local_sem=lsem)

    def signal(d, rsem):
        rid, pid = topo.addr(d, core)
        m = topo.mask(core, d)
        g.remote_sem_update(remote_sem=rsem, local_sem=S.lz, pid=pid, routing_id=rid, dma_engine_mask=m & -m)
        lz[0] += 1

    def loads(per):
        for c in range(n):
            if c:
                g.sync.wait_ge(S.xr, per * c)
            g.sync.dma_start(buf[0], xc(T.x, c)).then_inc(S.ld, 16)

    side = A if core in A else B
    on = _pop(topo.mask(core, [d for d in side if d != core][0]))
    xm = topo.mask(gB, gA[0])
    ex = _pop(xm)
    hi = topo.mask(gA[0], gA[1]) & ~xm
    eh = _pop(hi)

    if core in pA or core in pB:
        inA = core in pA
        pair = pA if inA else pB
        rinc = eh if inA else on
        loads(on)
        for c in range(n):
            p, k = c % 2, c // 2
            g.scalar.wait_ge(S["aR%d" % p], rinc * (k + 1))
            g.scalar.dma_start(xc(T.y, c), buf[2 + p]).then_inc(S["st%d" % p], 16)

        def contribute(c):
            p, k = c % 2, c // 2
            g.wait_ge(S.ld, 16 * (c + 1))
            if not inA and c >= 3:
                g.wait_ge(S["aR%d" % ((c - 3) % 2)], rinc * ((c - 3) // 2 + 1))
            if pair[p] == core:
                copy(0, pair[1 - p], 1, S.aL, S.xr)
                return
            g.wait_ge(S.aL, on * (k + 1))
            if inA:
                if c >= 2:
                    g.wait_ge(S.cL, k)
                fold([0, 1], gA[p], 1, S.aL, S.xr)
            else:
                fold([0, 1], gB, 1 + c % 3, S["aLX%d" % (c % 3)], S.xr)

        def credit(c):
            p, k = c % 2, c // 2
            g.wait_ge(S["st%d" % p], 16 * (k + 1))
            if c + 2 < n:
                signal(gA[p] if inA else gB, S["cR%d" % p])

        for c in range(n):
            plan("conA" if inA else "conB", c, contribute)
            plan("crA" if inA else "crB", c, credit)
        play()
        g.wait_ge(S.xr, on * n)
        g.wait_ge(S.lz, lz[0])
        return

    if core == gB:
        loads(ex)
        for c in range(n):
            j = c % 3
            g.scalar.wait_ge(S["aX%d" % j], ex * (c // 3 + 1))
            g.scalar.dma_start(xc(T.y, c), buf[1 + j]).then_inc(S["sx%d" % j], 16)

        def up(c):
            j = c % 3
            g.wait_ge(S.ld, 16 * (c + 1))
            g.wait_ge(S["aLX%d" % j], on * (c // 3 + 1))
            if c >= 2:
                g.wait_ge(S["aX%d" % ((c - 2) % 3)], ex * ((c - 2) // 3 + 1))
            fold([0, 1 + j], gA[1 - c % 2], 3, S.aSB, S.xr)

        def down(c):
            j, p = c % 3, c % 2
            g.wait_ge(S["sx%d" % j], 16 * (c // 3 + 1))
            if c >= 2:
                g.wait_ge(S["cR%d" % p], 2 * (c // 2))
            g.remote_dma_fused([RemoteDMATransfer(dst_ids=[did(d) for d in pB], dma_engine_mask=topo.mask(core, pB[0]),
                                                  remote_sem=S["aR%d" % p], srcs=[buf[1 + j]],
                                                  dsts=[buf[2 + p] for d in pB], alu_op=0)], local_sem=S.lz)
            lz[0] += on

        for c in range(n):
            plan("up", c, up)
            plan("down", c, down)
        play()
        g.wait_ge(S.xr, ex * n)
        g.wait_ge(S.lz, lz[0])
        return

    me = gA.index(core)
    other = gA[1 - me]
    loads(on)
    for c in range(n):
        p, k = c % 2, c // 2
        if p == me:
            g.scalar.wait_ge(S.aF, on * (k + 1))
            g.scalar.dma_start(xc(T.y, c), buf[1]).then_inc(S.stA, 16)
        else:
            g.scalar.wait_ge(S["aR%d" % p], eh * (k + 1))
            g.scalar.dma_start(xc(T.y, c), buf[2]).then_inc(S.stB, 16)

    def m2_fold(c):
        k = c // 2
        g.wait_ge(S.ld, 16 * (c + 1))
        g.wait_ge(S.aL, on * (k + 1))
        if c >= 2:
            g.wait_ge(S.cSA, k)
        fold([0, 1], other, 2, S.aSA, S.xr)

    def m2_spread(c):
        p, k = c % 2, c // 2
        g.wait_ge(S.aF, on * (k + 1))
        if c >= 2:
            g.wait_ge(S["cR%d" % p], 2 * k)
        g.remote_dma_fused([
            RemoteDMATransfer(dst_ids=[did(gB)], dma_engine_mask=topo.mask(core, gB), remote_sem=S["aX%d" % (c % 3)],
                              srcs=[buf[1]], dsts=[buf[1 + c % 3]], alu_op=0),
            RemoteDMATransfer(dst_ids=[did(pA[0]), did(pA[1]), did(other)], dma_engine_mask=hi,
                              remote_sem=S["aR%d" % p], srcs=[buf[1]], dsts=[buf[2 + p], buf[2 + p], buf[2]], alu_op=0),
        ], local_sem=S.bl)

    def m2_credit(c):
        k = c // 2
        g.wait_ge(S.stA, 16 * (k + 1))
        g.wait_ge(S.bl, (ex + eh) * (k + 1))
        if c + 2 < n:
            signal(pA[1 - c % 2], S.cL)

    def f_final(c):
        k = c // 2
        g.wait_ge(S.ld, 16 * (c + 1))
        g.wait_ge(S.aSA, on * (k + 1))
        g.wait_ge(S.aSB, ex * (k + 1))
        fold([0, 2, 3], other, 1, S.aF, S.xr)

    def f_credit(c):
        g.wait_ge(S.stB, 16 * (c // 2 + 1))
        if c + 2 < n:
            signal(other, S.cSA)

    for c in range(n):
        if c % 2 == me:
            plan("m2f", c, m2_fold)
            plan("spr", c, m2_spread)
            plan("cl", c, m2_credit)
        else:
            plan("fin", c, f_final)
            plan("cs", c, f_credit)
    play()
    g.wait_ge(S.xr, on * n)
    g.wait_ge(S.lz, lz[0])
